import numpy as np
import ml_dtypes


def mxq(x, axis, fmt="e4m3"):
    dtype, down = {"e4m3": (ml_dtypes.float8_e4m3fn, 7), "e5m2": (ml_dtypes.float8_e5m2, 14)}[fmt]
    v = np.moveaxis(np.asarray(x, np.float32).astype(ml_dtypes.bfloat16).astype(np.float64), axis, -1)
    blocks = v.reshape(v.shape[:-1] + (-1, 32))
    amax = np.abs(blocks).max(-1, keepdims=True)
    byte = np.maximum(np.where(amax > 0, np.frexp(amax)[1] - 1 + 127, 0) - down, 1)
    scale = np.exp2(byte - 127.0)
    codes = (blocks / scale).astype(np.float32).astype(dtype).astype(np.float64)
    return np.moveaxis((codes * scale).reshape(v.shape), -1, axis)


WIDE = False


def mx_kscale(k):
    if not WIDE:
        return np.ones(k)
    levels = np.array([10, -10, 5, -5, 0])
    if k % 512:
        return np.exp2(np.random.permutation(np.resize(levels, k // 32))).repeat(32)
    a = np.empty((k // 512, 16))
    for p in range(k // 512):
        a[p, :8] = np.random.permutation(np.resize(levels, 8))
        for g in range(8):
            far = levels[np.abs(levels - a[p, g]) >= 10]
            a[p, g + 8] = far[np.random.randint(len(far))]
    return np.exp2(a.ravel()).repeat(32)


def f64(x):
    return np.asarray(x).astype(np.float64)


def striped(idx):
    return np.tile(idx.reshape(-1, 16).T, (8, 1)).astype(np.uint16)


def unstriped(offs):
    return offs[:16].T.reshape(-1).astype(np.int64)


def pack_weight(w):
    k, n = w.shape
    w = f64(np.asarray(w, np.float32).astype(ml_dtypes.bfloat16)).reshape(k // 32, 32, n)
    amax = np.abs(w).max(1)
    byte = np.clip(np.where(amax > 0, np.frexp(amax)[1] - 1 + 127 - 7, 1), 1, 254)
    scaled = (w * np.exp2(127.0 - byte)[:, None, :]).reshape(k, n).astype(np.float32)
    words = np.ascontiguousarray(scaled.reshape(k // 512, 128, 4, n).transpose(0, 1, 3, 2)).astype(ml_dtypes.float8_e4m3fn).view(np.uint8)
    return words, np.ascontiguousarray(byte.astype(np.uint8).reshape(k // 512, 16, n))


def unpack_weight(words, scales):
    g, p, n, _ = words.shape
    vals = np.ascontiguousarray(words).view(ml_dtypes.float8_e4m3fn).astype(np.float64) * np.repeat(np.exp2(scales.astype(np.float64) - 127.0), 8, axis=1)[..., None]
    return vals.transpose(0, 1, 3, 2).reshape(g * 512, n)


def relu(v):
    return np.maximum(v, 0.0)


K, T, S, D, V, N = 1024, 1024, 512, 3, 256, 128
P = 2 ** 7


def setup_inputs():
    n = np.random.standard_normal
    s = mx_kscale(K)[:, None]
    packed_w1 = pack_weight(n((K, N)) / np.sqrt(K) / s)
    return {
        "xT": (n((K, T)) * s).astype(np.float32),
        "w1_words": packed_w1[0],
        "w1_scales": packed_w1[1],
        "gate": (np.tile(np.random.uniform(0.2, 1.0, (D, 1, V)) / np.sqrt(D), (1, P, 1))).astype(np.float32),
        "offs": striped(np.random.permutation(T)[:S]),
        "cen": striped(np.random.permutation(S)[:V]),
        "pos1": striped(np.random.permutation(S)[:V]),
        "pos2": striped(np.random.permutation(S)[:V]),
        "pos3": striped(np.random.permutation(S)[:V]),
    }


def reference(xT, w1_words, w1_scales, gate, offs, cen, pos1, pos2, pos3):
    xq = mxq(f64(xT)[:, unstriped(offs)], 0, "e4m3")
    y = relu(unpack_weight(w1_words, w1_scales).T @ xq)
    yc = y[:, unstriped(cen)]
    return yc + (y[:, unstriped(pos1)] - yc) * f64(gate)[0, :1] + (y[:, unstriped(pos2)] - yc) * f64(gate)[1, :1] + (y[:, unstriped(pos3)] - yc) * f64(gate)[2, :1]

@@ -1,0 +1,158 @@
+from contextlib import ExitStack
+
+import concourse.mybir as mybir
+
+K, T, S, D, V, N = 1024, 1024, 512, 3, 256, 128
+P = 128
+PACK = 4
+K_PASS = P * PACK
+PASSES = K // K_PASS
+LANES = 16
+
+FLOPS = 2 * K * S * N
+
+F32 = mybir.dt.float32
+BF16 = mybir.dt.bfloat16
+U32 = mybir.dt.uint32
+I32 = mybir.dt.int32
+U16 = mybir.dt.uint16
+U8 = mybir.dt.uint8
+FP8X4 = mybir.dt.float8_e4m3fn_x4
+ALU = mybir.AluOpType
+ACT = mybir.ActivationFunctionType
+
+HALF = T // 2
+VECTOR_TOKENS = 320
+PIECES = ((0, 256), (256, 384), (384, 512))
+
+
+def tile_picked_grand_relu_e_kernel(
+    tc, xT, w1_words, w1_scales, gate, offs, cen, pos1, pos2, pos3, out
+):
+    nc = tc.nc
+    with ExitStack() as ctx:
+        keep = ctx.enter_context(tc.tile_pool(name="keep", bufs=1))
+        psum = ctx.enter_context(tc.psum_pool(name="psum", bufs=1))
+
+        offs_sb = keep.tile([P, S // LANES], U16, name="offs_sb")
+        cen_sb = keep.tile([P, V // LANES], U16, name="cen_sb")
+        pos_sb = [keep.tile([P, V // LANES], U16, name=f"pos_sb{d}") for d in range(D)]
+        w_words = keep.tile([P, PASSES, N], U32, name="w_words", align_bytes=64)
+        w_scales = keep.tile([P, PASSES, N], U8, name="w_scales", align_bytes=64)
+        gate_sb = keep.tile([P, D, V], F32, name="gate_sb")
+
+        nc.gpsimd.memset(w_scales[:], 0)
+
+        x_rows = xT.rearrange("(z p u e) t -> z u p e t", z=PASSES, p=P, u=2, e=2)
+        raw = {}
+        for z in range(PASSES):
+            for u in range(2):
+                for h in range(2):
+                    raw[z, u, h] = keep.tile([P, 2, HALF], F32, name=f"raw{z}{u}{h}")
+                    nc.sync.dma_start(out=raw[z, u, h][:], in_=x_rows[z, u, :, :, h * HALF : (h + 1) * HALF])
+                if (z, u) == (0, 0):
+                    nc.sync.dma_start(out=offs_sb[:], in_=offs)
+        nc.sync.dma_start(
+            out=w_words[:].bitcast(I32), in_=w1_words.rearrange("z p n r -> p z (n r)").bitcast(I32)
+        )
+        for q in range(4):
+            nc.sync.dma_start(
+                out=w_scales[32 * q : 32 * q + 4, :, :].bitcast(I32),
+                in_=w1_scales[:, 4 * q : 4 * q + 4, :].rearrange("z r n -> r z n").bitcast(I32),
+            )
+        nc.sync.dma_start(out=gate_sb[:], in_=gate.rearrange("d p v -> p d v"))
+        for tile, src in zip(pos_sb + [cen_sb], (pos1, pos2, pos3, cen)):
+            nc.sync.dma_start(out=tile[:], in_=src)
+
+        def round_pairs(z, u):
+            pairs = keep.tile([P, T, 2], BF16, name=f"pairs{z}{u}", align_bytes=64)
+            first = raw[z, u, 0][:].rearrange("p e t -> p t e")
+            second = raw[z, u, 1][:].rearrange("p e t -> p t e")
+            cut = HALF - VECTOR_TOKENS
+            nc.scalar.activation(out=pairs[:, 0:HALF, :], in_=first, func=ACT.Copy)
+            nc.scalar.activation(out=pairs[:, HALF : HALF + cut, :], in_=second[:, 0:cut, :], func=ACT.Copy)
+            nc.vector.tensor_copy(out=pairs[:, HALF + cut : T, :], in_=second[:, cut:HALF, :])
+            return pairs[:].rearrange("p t e -> p (t e)").bitcast(U32)
+
+        def pick(window, picked, u, lo, hi):
+            words = picked[:].bitcast(U32).rearrange("p (j u) -> p j u", u=2)
+            nc.vector.tensor_copy(out=words[:, :, u], in_=window.indirect(offs_sb[:, lo // LANES : hi // LANES]))
+
+        def quantize(picked, name):
+            width = picked.shape[1] // PACK
+            codes = keep.tile([P, width], U32, name=f"codes{name}", align_bytes=64)
+            scales = keep.tile([P, width], U8, name=f"scales{name}", align_bytes=64)
+            nc.vector.quantize_mx(out=codes[:].bitcast(FP8X4), scales=scales[:], in_=picked[:])
+            return codes, scales
+
+        def multiply(acc, z, codes, scales):
+            nc.tensor.matmul_mx(
+                out=acc[:],
+                lhsT=w_words[:, z, :].bitcast(FP8X4),
+                lhsT_scale=w_scales[:, z, :],
+                rhs=codes.bitcast(FP8X4),
+                rhs_scale=scales,
+                start=(z == 0),
+                stop=(z == PASSES - 1),
+            )
+
+        accs = [psum.tile([N, hi - lo], F32, name=f"acc{lo}") for lo, hi in PIECES]
+
+        picked0 = keep.tile([P, S * PACK], BF16, name="picked0", align_bytes=64)
+        for u in range(2):
+            pick(round_pairs(0, u), picked0, u, 0, S)
+        codes0, scales0 = quantize(picked0, "0")
+        for acc, (lo, hi) in zip(accs, PIECES):
+            multiply(acc, 0, codes0[:, lo:hi], scales0[:, lo:hi])
+
+        picked1 = [
+            keep.tile([P, (hi - lo) * PACK], BF16, name=f"picked1_{lo}", align_bytes=64) for lo, hi in PIECES
+        ]
+        window = round_pairs(1, 0)
+        for picked, (lo, hi) in zip(picked1, PIECES):
+            pick(window, picked, 0, lo, hi)
+        window = round_pairs(1, 1)
+        y = keep.tile([N, S], F32, name="y")
+
+        def finish(i):
+            lo, hi = PIECES[i]
+            codes, scales = quantize(picked1[i], f"1_{lo}")
+            multiply(accs[i], 1, codes[:], scales[:])
+            nc.scalar.activation(out=y[:, lo:hi], in_=accs[i][:], func=ACT.Relu)
+
+        for i, (lo, hi) in enumerate(PIECES):
+            pick(window, picked1[i], 1, lo, hi)
+            if i > 0:
+                finish(i - 1)
+        finish(len(PIECES) - 1)
+
+        minus01 = keep.tile([P, V], F32, name="minus01")
+        stay = keep.tile([P, V], F32, name="stay")
+        nc.vector.scalar_tensor_tensor(
+            out=minus01[:], in0=gate_sb[:, 0, :], scalar=-1.0, in1=gate_sb[:, 1, :], op0=ALU.mult, op1=ALU.subtract
+        )
+        nc.vector.scalar_tensor_tensor(
+            out=stay[:], in0=minus01[:], scalar=1.0, in1=gate_sb[:, 2, :], op0=ALU.add, op1=ALU.subtract
+        )
+
+        terms = [keep.tile([N, V], F32, name=f"term{d}") for d in range(D)]
+        for d in range(D):
+            nc.vector.tensor_tensor(out=terms[d][:], in0=y[:].indirect(pos_sb[d][:]), in1=gate_sb[:, d, :], op=ALU.mult)
+        sum01 = keep.tile([N, V], F32, name="sum01")
+        sum012 = keep.tile([N, V], F32, name="sum012")
+        own = [keep.tile([N, V // 2], F32, name=f"own{h}") for h in range(2)]
+        res = keep.tile([N, V], F32, name="res")
+
+        def centre(h):
+            cols = slice(h * (V // 2), (h + 1) * (V // 2))
+            lists = cen_sb[:, h * (V // 2 // LANES) : (h + 1) * (V // 2 // LANES)]
+            nc.vector.tensor_tensor(out=own[h][:], in0=y[:].indirect(lists), in1=stay[:, cols], op=ALU.mult)
+
+        nc.vector.tensor_tensor(out=sum01[:], in0=terms[0][:], in1=terms[1][:], op=ALU.add)
+        centre(0)
+        nc.vector.tensor_tensor(out=sum012[:], in0=sum01[:], in1=terms[2][:], op=ALU.add)
+        centre(1)
+        for h in range(2):
+            cols = slice(h * (V // 2), (h + 1) * (V // 2))
+            nc.vector.tensor_tensor(out=res[:, cols], in0=sum012[:, cols], in1=own[h][:], op=ALU.add)
+        nc.sync.dma_start(out=out, in_=res[:])

@@ -22,8 +22,13 @@ ALU = mybir.AluOpType
 ACT = mybir.ActivationFunctionType
 
 HALF = T // 2
-VECTOR_TOKENS = 320
-PIECES = ((0, 256), (256, 384), (384, 512))
+CHUNKS = {
+    (0, 0): ((0, 344, T),),
+    (0, 1): ((0, HALF, HALF), (HALF, HALF + 176, T)),
+    (1, 0): ((0, HALF, HALF), (HALF, T, T)),
+    (1, 1): ((0, HALF, HALF), (HALF, HALF + 224, T)),
+}
+PIECES = ((0, 128), (128, 256), (256, 384), (384, 512))
 
 
 def tile_picked_grand_relu_e_kernel(
@@ -47,9 +52,9 @@ def tile_picked_grand_relu_e_kernel(
         raw = {}
         for z in range(PASSES):
             for u in range(2):
-                for h in range(2):
-                    raw[z, u, h] = keep.tile([P, 2, HALF], F32, name=f"raw{z}{u}{h}")
-                    nc.sync.dma_start(out=raw[z, u, h][:], in_=x_rows[z, u, :, :, h * HALF : (h + 1) * HALF])
+                for lo, cut, hi in CHUNKS[z, u]:
+                    raw[z, u, lo] = keep.tile([P, 2, hi - lo], F32, name=f"raw{z}{u}_{lo}")
+                    nc.sync.dma_start(out=raw[z, u, lo][:], in_=x_rows[z, u, :, :, lo:hi])
                 if (z, u) == (0, 0):
                     nc.sync.dma_start(out=offs_sb[:], in_=offs)
         nc.sync.dma_start(
@@ -66,17 +71,31 @@ def tile_picked_grand_relu_e_kernel(
 
         def round_pairs(z, u):
             pairs = keep.tile([P, T, 2], BF16, name=f"pairs{z}{u}", align_bytes=64)
-            first = raw[z, u, 0][:].rearrange("p e t -> p t e")
-            second = raw[z, u, 1][:].rearrange("p e t -> p t e")
-            cut = HALF - VECTOR_TOKENS
-            nc.scalar.activation(out=pairs[:, 0:HALF, :], in_=first, func=ACT.Copy)
-            nc.scalar.activation(out=pairs[:, HALF : HALF + cut, :], in_=second[:, 0:cut, :], func=ACT.Copy)
-            nc.vector.tensor_copy(out=pairs[:, HALF + cut : T, :], in_=second[:, cut:HALF, :])
+            for lo, cut, hi in CHUNKS[z, u]:
+                rows = raw[z, u, lo][:].rearrange("p e t -> p t e")
+                nc.scalar.activation(out=pairs[:, lo:cut, :], in_=rows[:, 0 : cut - lo, :], func=ACT.Copy)
+                if cut < hi:
+                    nc.vector.tensor_copy(out=pairs[:, cut:hi, :], in_=rows[:, cut - lo : hi - lo, :])
             return pairs[:].rearrange("p t e -> p (t e)").bitcast(U32)
 
         def pick(window, picked, u, lo, hi):
-            words = picked[:].bitcast(U32).rearrange("p (j u) -> p j u", u=2)
-            nc.vector.tensor_copy(out=words[:, :, u], in_=window.indirect(offs_sb[:, lo // LANES : hi // LANES]))
+            nc.vector.tensor_copy(out=picked[:, u, :], in_=window.indirect(offs_sb[:, lo // LANES : hi // LANES]))
+
+        def weave(picked, name, on_scalar, woven=None):
+            width = picked.shape[2]
+            if woven is None:
+                woven = keep.tile([P, width * PACK], BF16, name=f"woven{name}", tag=f"woven{name}", align_bytes=64)
+            if on_scalar:
+                nc.scalar.copy(
+                    out=woven[:].bitcast(U32).rearrange("p (j u) -> p j u", u=2),
+                    in_=picked.rearrange("p u j -> p j u"),
+                )
+            else:
+                nc.vector.tensor_copy(
+                    out=woven[:].bitcast(I32).rearrange("p (j u) -> p j u", u=2),
+                    in_=picked[:].bitcast(I32).rearrange("p u j -> p j u"),
+                )
+            return woven
 
         def quantize(picked, name):
             width = picked.shape[1] // PACK
@@ -98,35 +117,44 @@ def tile_picked_grand_relu_e_kernel(
 
         accs = [psum.tile([N, hi - lo], F32, name=f"acc{lo}") for lo, hi in PIECES]
 
-        picked0 = keep.tile([P, S * PACK], BF16, name="picked0", align_bytes=64)
+        halves = ((0, S // 2), (S // 2, S))
+        picked0 = [keep.tile([P, 2, hi - lo], U32, name=f"picked0_{lo}") for lo, hi in halves]
         for u in range(2):
-            pick(round_pairs(0, u), picked0, u, 0, S)
-        codes0, scales0 = quantize(picked0, "0")
+            window = round_pairs(0, u)
+            for picked, (lo, hi) in zip(picked0, halves):
+                pick(window, picked, u, lo, hi)
+        woven0 = [weave(picked, f"0_{lo}", False) for picked, (lo, hi) in zip(picked0, halves)]
+        quantized0 = [quantize(woven, f"0_{lo}") for woven, (lo, hi) in zip(woven0, halves)]
         for acc, (lo, hi) in zip(accs, PIECES):
-            multiply(acc, 0, codes0[:, lo:hi], scales0[:, lo:hi])
+            codes0, scales0 = quantized0[lo // (S // 2)]
+            cols = slice(lo % (S // 2), lo % (S // 2) + hi - lo)
+            multiply(acc, 0, codes0[:, cols], scales0[:, cols])
 
-        picked1 = [
-            keep.tile([P, (hi - lo) * PACK], BF16, name=f"picked1_{lo}", align_bytes=64) for lo, hi in PIECES
-        ]
-        window = round_pairs(1, 0)
-        for picked, (lo, hi) in zip(picked1, PIECES):
-            pick(window, picked, 0, lo, hi)
-        window = round_pairs(1, 1)
+        last_lo, last_hi = PIECES[-1]
+        picked1 = [keep.tile([P, 2, hi - lo], U32, name=f"picked1_{lo}") for lo, hi in PIECES[:-1]]
+        woven_end = keep.tile([P, 256 * PACK], BF16, name="woven_end", tag="woven_end", align_bytes=64)
+        last_rows = woven_end[:, 128 * PACK :].bitcast(U32).rearrange("p (j u) -> p u j", u=2)
+        for u in range(2):
+            window = round_pairs(1, u)
+            for picked, (lo, hi) in zip(picked1 + [last_rows], PIECES):
+                pick(window, picked, u, lo, hi)
         y = keep.tile([N, S], F32, name="y")
 
-        def finish(i):
+        def finish(i, codes, scales):
             lo, hi = PIECES[i]
-            codes, scales = quantize(picked1[i], f"1_{lo}")
-            multiply(accs[i], 1, codes[:], scales[:])
+            multiply(accs[i], 1, codes, scales)
             nc.scalar.activation(out=y[:, lo:hi], in_=accs[i][:], func=ACT.Relu)
 
-        for i, (lo, hi) in enumerate(PIECES):
-            pick(window, picked1[i], 1, lo, hi)
-            if i > 0:
-                finish(i - 1)
-        finish(len(PIECES) - 1)
+        woven1 = [weave(picked1[i][:], f"1_{i}", True) for i in range(2)]
+        weave(picked1[2][:], "", True, woven_end[:, 0 : 128 * PACK])
+        for i in range(2):
+            codes, scales = quantize(woven1[i], f"1_{i}")
+            finish(i, codes[:], scales[:])
+        codes, scales = quantize(woven_end, "1_end")
+        for i in range(2):
+            finish(2 + i, codes[:, 128 * i : 128 * (i + 1)], scales[:, 128 * i : 128 * (i + 1)])
 
-        minus01 = keep.tile([P, V], F32, name="minus01")
+        minus01 = keep.tile([P, V], F32, name="minus01", tag="woven_end", align_bytes=64)
         stay = keep.tile([P, V], F32, name="stay")
         nc.vector.scalar_tensor_tensor(
             out=minus01[:], in0=gate_sb[:, 0, :], scalar=-1.0, in1=gate_sb[:, 1, :], op0=ALU.mult, op1=ALU.subtract

@@ -23,10 +23,10 @@ ACT = mybir.ActivationFunctionType
 
 HALF = T // 2
 CHUNKS = {
-    (0, 0): ((0, 344, T),),
-    (0, 1): ((0, HALF, HALF), (HALF, HALF + 176, T)),
+    (0, 0): ((0, 384, T),),
+    (0, 1): ((0, 384, T),),
     (1, 0): ((0, HALF, HALF), (HALF, T, T)),
-    (1, 1): ((0, HALF, HALF), (HALF, HALF + 224, T)),
+    (1, 1): ((0, HALF, HALF), (HALF, HALF + 240, T)),
 }
 PIECES = ((0, 128), (128, 256), (256, 384), (384, 512))
 
@@ -131,13 +131,17 @@ def tile_picked_grand_relu_e_kernel(
             multiply(acc, 0, codes0[:, cols], scales0[:, cols])
 
         last_lo, last_hi = PIECES[-1]
-        picked1 = [keep.tile([P, 2, hi - lo], U32, name=f"picked1_{lo}") for lo, hi in PIECES[:-1]]
+        picked1_tile = keep.tile([P, 2 * last_lo], U32, name="picked1")
+        picked1_rows = picked1_tile[:].rearrange("p (u j) -> p u j", u=2)
+        picked1 = [picked1_rows[:, :, lo:hi] for lo, hi in PIECES[:-1]]
         woven_end = keep.tile([P, 256 * PACK], BF16, name="woven_end", tag="woven_end", align_bytes=64)
         last_rows = woven_end[:, 128 * PACK :].bitcast(U32).rearrange("p (j u) -> p u j", u=2)
-        for u in range(2):
-            window = round_pairs(1, u)
-            for picked, (lo, hi) in zip(picked1 + [last_rows], PIECES):
-                pick(window, picked, u, lo, hi)
+        window = round_pairs(1, 0)
+        pick(window, picked1_rows, 0, 0, last_lo)
+        pick(window, last_rows, 0, last_lo, last_hi)
+        window = round_pairs(1, 1)
+        for picked, (lo, hi) in zip(picked1 + [last_rows], PIECES):
+            pick(window, picked, 1, lo, hi)
         y = keep.tile([N, S], F32, name="y")
 
         def finish(i, codes, scales):
@@ -145,8 +149,8 @@ def tile_picked_grand_relu_e_kernel(
             multiply(accs[i], 1, codes, scales)
             nc.scalar.activation(out=y[:, lo:hi], in_=accs[i][:], func=ACT.Relu)
 
-        woven1 = [weave(picked1[i][:], f"1_{i}", True) for i in range(2)]
-        weave(picked1[2][:], "", True, woven_end[:, 0 : 128 * PACK])
+        woven1 = [weave(picked1[i], f"1_{i}", True) for i in range(2)]
+        weave(picked1[2], "", True, woven_end[:, 0 : 128 * PACK])
         for i in range(2):
             codes, scales = quantize(woven1[i], f"1_{i}")
             finish(i, codes[:], scales[:])
@@ -169,7 +173,6 @@ def tile_picked_grand_relu_e_kernel(
         sum01 = keep.tile([N, V], F32, name="sum01")
         sum012 = keep.tile([N, V], F32, name="sum012")
         own = [keep.tile([N, V // 2], F32, name=f"own{h}") for h in range(2)]
-        res = keep.tile([N, V], F32, name="res")
 
         def centre(h):
             cols = slice(h * (V // 2), (h + 1) * (V // 2))
@@ -180,7 +183,8 @@ def tile_picked_grand_relu_e_kernel(
         centre(0)
         nc.vector.tensor_tensor(out=sum012[:], in0=sum01[:], in1=terms[2][:], op=ALU.add)
         centre(1)
-        for h in range(2):
+        for h, queue in enumerate((nc.scalar, nc.sync)):
             cols = slice(h * (V // 2), (h + 1) * (V // 2))
-            nc.vector.tensor_tensor(out=res[:, cols], in0=sum012[:, cols], in1=own[h][:], op=ALU.add)
-        nc.sync.dma_start(out=out, in_=res[:])
+            res = keep.tile([N, V // 2], F32, name=f"res{h}")
+            nc.vector.tensor_tensor(out=res[:], in0=sum012[:, cols], in1=own[h][:], op=ALU.add)
+            queue.dma_start(out=out[:, cols], in_=res[:])

from contextlib import ExitStack

import concourse.mybir as mybir

K, T, S, D, V, N = 1024, 1024, 512, 3, 256, 128
P = 128
PACK = 4
K_PASS = P * PACK
PASSES = K // K_PASS
LANES = 16

FLOPS = 2 * K * S * N

F32 = mybir.dt.float32
BF16 = mybir.dt.bfloat16
U32 = mybir.dt.uint32
I32 = mybir.dt.int32
U16 = mybir.dt.uint16
U8 = mybir.dt.uint8
FP8X4 = mybir.dt.float8_e4m3fn_x4
ALU = mybir.AluOpType
ACT = mybir.ActivationFunctionType

HALF = T // 2
CHUNKS = {
    (0, 0): ((0, 384, T),),
    (0, 1): ((0, 384, T),),
    (1, 0): ((0, HALF, HALF), (HALF, T, T)),
    (1, 1): ((0, HALF, HALF), (HALF, HALF + 240, T)),
}
PIECES = ((0, 128), (128, 256), (256, 384), (384, 512))


def tile_picked_grand_relu_e_kernel(
    tc, xT, w1_words, w1_scales, gate, offs, cen, pos1, pos2, pos3, out
):
    nc = tc.nc
    with ExitStack() as ctx:
        keep = ctx.enter_context(tc.tile_pool(name="keep", bufs=1))
        psum = ctx.enter_context(tc.psum_pool(name="psum", bufs=1))

        offs_sb = keep.tile([P, S // LANES], U16, name="offs_sb")
        cen_sb = keep.tile([P, V // LANES], U16, name="cen_sb")
        pos_sb = [keep.tile([P, V // LANES], U16, name=f"pos_sb{d}") for d in range(D)]
        w_words = keep.tile([P, PASSES, N], U32, name="w_words", align_bytes=64)
        w_scales = keep.tile([P, PASSES, N], U8, name="w_scales", align_bytes=64)
        gate_sb = keep.tile([P, D, V], F32, name="gate_sb")

        nc.gpsimd.memset(w_scales[:], 0)

        x_rows = xT.rearrange("(z p u e) t -> z u p e t", z=PASSES, p=P, u=2, e=2)
        raw = {}
        for z in range(PASSES):
            for u in range(2):
                for lo, cut, hi in CHUNKS[z, u]:
                    raw[z, u, lo] = keep.tile([P, 2, hi - lo], F32, name=f"raw{z}{u}_{lo}")
                    nc.sync.dma_start(out=raw[z, u, lo][:], in_=x_rows[z, u, :, :, lo:hi])
                if (z, u) == (0, 0):
                    nc.sync.dma_start(out=offs_sb[:], in_=offs)
        nc.sync.dma_start(
            out=w_words[:].bitcast(I32), in_=w1_words.rearrange("z p n r -> p z (n r)").bitcast(I32)
        )
        for q in range(4):
            nc.sync.dma_start(
                out=w_scales[32 * q : 32 * q + 4, :, :].bitcast(I32),
                in_=w1_scales[:, 4 * q : 4 * q + 4, :].rearrange("z r n -> r z n").bitcast(I32),
            )
        nc.sync.dma_start(out=gate_sb[:], in_=gate.rearrange("d p v -> p d v"))
        for tile, src in zip(pos_sb + [cen_sb], (pos1, pos2, pos3, cen)):
            nc.sync.dma_start(out=tile[:], in_=src)

        def round_pairs(z, u):
            pairs = keep.tile([P, T, 2], BF16, name=f"pairs{z}{u}", align_bytes=64)
            for lo, cut, hi in CHUNKS[z, u]:
                rows = raw[z, u, lo][:].rearrange("p e t -> p t e")
                nc.scalar.activation(out=pairs[:, lo:cut, :], in_=rows[:, 0 : cut - lo, :], func=ACT.Copy)
                if cut < hi:
                    nc.vector.tensor_copy(out=pairs[:, cut:hi, :], in_=rows[:, cut - lo : hi - lo, :])
            return pairs[:].rearrange("p t e -> p (t e)").bitcast(U32)

        def pick(window, picked, u, lo, hi):
            nc.vector.tensor_copy(out=picked[:, u, :], in_=window.indirect(offs_sb[:, lo // LANES : hi // LANES]))

        def weave(picked, name, on_scalar, woven=None):
            width = picked.shape[2]
            if woven is None:
                woven = keep.tile([P, width * PACK], BF16, name=f"woven{name}", tag=f"woven{name}", align_bytes=64)
            if on_scalar:
                nc.scalar.copy(
                    out=woven[:].bitcast(U32).rearrange("p (j u) -> p j u", u=2),
                    in_=picked.rearrange("p u j -> p j u"),
                )
            else:
                nc.vector.tensor_copy(
                    out=woven[:].bitcast(I32).rearrange("p (j u) -> p j u", u=2),
                    in_=picked[:].bitcast(I32).rearrange("p u j -> p j u"),
                )
            return woven

        def quantize(picked, name):
            width = picked.shape[1] // PACK
            codes = keep.tile([P, width], U32, name=f"codes{name}", align_bytes=64)
            scales = keep.tile([P, width], U8, name=f"scales{name}", align_bytes=64)
            nc.vector.quantize_mx(out=codes[:].bitcast(FP8X4), scales=scales[:], in_=picked[:])
            return codes, scales

        def multiply(acc, z, codes, scales):
            nc.tensor.matmul_mx(
                out=acc[:],
                lhsT=w_words[:, z, :].bitcast(FP8X4),
                lhsT_scale=w_scales[:, z, :],
                rhs=codes.bitcast(FP8X4),
                rhs_scale=scales,
                start=(z == 0),
                stop=(z == PASSES - 1),
            )

        accs = [psum.tile([N, hi - lo], F32, name=f"acc{lo}") for lo, hi in PIECES]

        halves = ((0, S // 2), (S // 2, S))
        picked0 = [keep.tile([P, 2, hi - lo], U32, name=f"picked0_{lo}") for lo, hi in halves]
        for u in range(2):
            window = round_pairs(0, u)
            for picked, (lo, hi) in zip(picked0, halves):
                pick(window, picked, u, lo, hi)
        woven0 = [weave(picked, f"0_{lo}", False) for picked, (lo, hi) in zip(picked0, halves)]
        quantized0 = [quantize(woven, f"0_{lo}") for woven, (lo, hi) in zip(woven0, halves)]
        for acc, (lo, hi) in zip(accs, PIECES):
            codes0, scales0 = quantized0[lo // (S // 2)]
            cols = slice(lo % (S // 2), lo % (S // 2) + hi - lo)
            multiply(acc, 0, codes0[:, cols], scales0[:, cols])

        last_lo, last_hi = PIECES[-1]
        picked1_tile = keep.tile([P, 2 * last_lo], U32, name="picked1")
        picked1_rows = picked1_tile[:].rearrange("p (u j) -> p u j", u=2)
        picked1 = [picked1_rows[:, :, lo:hi] for lo, hi in PIECES[:-1]]
        woven_end = keep.tile([P, 256 * PACK], BF16, name="woven_end", tag="woven_end", align_bytes=64)
        last_rows = woven_end[:, 128 * PACK :].bitcast(U32).rearrange("p (j u) -> p u j", u=2)
        window = round_pairs(1, 0)
        pick(window, picked1_rows, 0, 0, last_lo)
        pick(window, last_rows, 0, last_lo, last_hi)
        window = round_pairs(1, 1)
        for picked, (lo, hi) in zip(picked1 + [last_rows], PIECES):
            pick(window, picked, 1, lo, hi)
        y = keep.tile([N, S], F32, name="y")

        def finish(i, codes, scales):
            lo, hi = PIECES[i]
            multiply(accs[i], 1, codes, scales)
            nc.scalar.activation(out=y[:, lo:hi], in_=accs[i][:], func=ACT.Relu)

        woven1 = [weave(picked1[i], f"1_{i}", True) for i in range(2)]
        weave(picked1[2], "", True, woven_end[:, 0 : 128 * PACK])
        for i in range(2):
            codes, scales = quantize(woven1[i], f"1_{i}")
            finish(i, codes[:], scales[:])
        codes, scales = quantize(woven_end, "1_end")
        for i in range(2):
            finish(2 + i, codes[:, 128 * i : 128 * (i + 1)], scales[:, 128 * i : 128 * (i + 1)])

        minus01 = keep.tile([P, V], F32, name="minus01", tag="woven_end", align_bytes=64)
        stay = keep.tile([P, V], F32, name="stay")
        nc.vector.scalar_tensor_tensor(
            out=minus01[:], in0=gate_sb[:, 0, :], scalar=-1.0, in1=gate_sb[:, 1, :], op0=ALU.mult, op1=ALU.subtract
        )
        nc.vector.scalar_tensor_tensor(
            out=stay[:], in0=minus01[:], scalar=1.0, in1=gate_sb[:, 2, :], op0=ALU.add, op1=ALU.subtract
        )

        terms = [keep.tile([N, V], F32, name=f"term{d}") for d in range(D)]
        for d in range(D):
            nc.vector.tensor_tensor(out=terms[d][:], in0=y[:].indirect(pos_sb[d][:]), in1=gate_sb[:, d, :], op=ALU.mult)
        sum01 = keep.tile([N, V], F32, name="sum01")
        sum012 = keep.tile([N, V], F32, name="sum012")
        own = [keep.tile([N, V // 2], F32, name=f"own{h}") for h in range(2)]

        def centre(h):
            cols = slice(h * (V // 2), (h + 1) * (V // 2))
            lists = cen_sb[:, h * (V // 2 // LANES) : (h + 1) * (V // 2 // LANES)]
            nc.vector.tensor_tensor(out=own[h][:], in0=y[:].indirect(lists), in1=stay[:, cols], op=ALU.mult)

        nc.vector.tensor_tensor(out=sum01[:], in0=terms[0][:], in1=terms[1][:], op=ALU.add)
        centre(0)
        nc.vector.tensor_tensor(out=sum012[:], in0=sum01[:], in1=terms[2][:], op=ALU.add)
        centre(1)
        for h, queue in enumerate((nc.scalar, nc.sync)):
            cols = slice(h * (V // 2), (h + 1) * (V // 2))
            res = keep.tile([N, V // 2], F32, name=f"res{h}")
            nc.vector.tensor_tensor(out=res[:], in0=sum012[:, cols], in1=own[h][:], op=ALU.add)
            queue.dma_start(out=out[:, cols], in_=res[:])
